import numpy as np
import ml_dtypes


def mxq(x, axis, fmt="e4m3"):
    dtype, down = {"e4m3": (ml_dtypes.float8_e4m3fn, 7), "e5m2": (ml_dtypes.float8_e5m2, 14)}[fmt]
    v = np.moveaxis(np.asarray(x, np.float32).astype(ml_dtypes.bfloat16).astype(np.float64), axis, -1)
    blocks = v.reshape(v.shape[:-1] + (-1, 32))
    amax = np.abs(blocks).max(-1, keepdims=True)
    byte = np.maximum(np.where(amax > 0, np.frexp(amax)[1] - 1 + 127, 0) - down, 1)
    scale = np.exp2(byte - 127.0)
    codes = (blocks / scale).astype(np.float32).astype(dtype).astype(np.float64)
    return np.moveaxis((codes * scale).reshape(v.shape), -1, axis)


WIDE = False


def mx_kscale(k):
    if not WIDE:
        return np.ones(k)
    levels = np.array([10, -10, 5, -5, 0])
    if k % 512:
        return np.exp2(np.random.permutation(np.resize(levels, k // 32))).repeat(32)
    a = np.empty((k // 512, 16))
    for p in range(k // 512):
        a[p, :8] = np.random.permutation(np.resize(levels, 8))
        for g in range(8):
            far = levels[np.abs(levels - a[p, g]) >= 10]
            a[p, g + 8] = far[np.random.randint(len(far))]
    return np.exp2(a.ravel()).repeat(32)


BF16 = ml_dtypes.bfloat16


def bf(x):
    return np.asarray(x, np.float32).astype(BF16)


def f64(x):
    return np.asarray(x).astype(np.float64)


E2M1 = np.array([0.0, 0.5, 1.0, 1.5, 2.0, 3.0, 4.0, 6.0, -0.0, -0.5, -1.0, -1.5, -2.0, -3.0, -4.0, -6.0])


def pack_weight(w, fmt):
    k, n = w.shape
    w = f64(bf(w)).reshape(k // 32, 32, n)
    amax = np.abs(w).max(1)
    if fmt == "e4m3":
        byte = np.frexp(amax)[1] - 1 + 127 - 7
    else:
        mant, ex = np.frexp(amax / 6.0)
        byte = np.where(mant > 0.5, ex, ex - 1) + 127
    byte = np.clip(np.where(amax > 0, byte, 1), 1, 254)
    scaled = (w * np.exp2(127.0 - byte)[:, None, :]).reshape(k, n).astype(np.float32)
    by_word = np.ascontiguousarray(scaled.reshape(k // 512, 128, 4, n).transpose(0, 1, 3, 2))
    if fmt == "e4m3":
        words = by_word.astype(ml_dtypes.float8_e4m3fn).view(np.uint8)
    else:
        c = by_word.astype(ml_dtypes.float4_e2m1fn).view(np.uint8) & 0xF
        words = c[..., 0::2] | (c[..., 1::2] << 4)
    return np.ascontiguousarray(words), np.ascontiguousarray(byte.astype(np.uint8).reshape(k // 512, 16, n))


def unpack_weight(words, scales, fmt):
    g, p, n, _ = words.shape
    if fmt == "e4m3":
        vals = np.ascontiguousarray(words).view(ml_dtypes.float8_e4m3fn).astype(np.float64)
    else:
        nib = np.empty((g, p, n, 4), np.uint8)
        nib[..., 0::2] = words & 0xF
        nib[..., 1::2] = words >> 4
        vals = E2M1[nib]
    vals = vals * np.repeat(np.exp2(scales.astype(np.float64) - 127.0), 8, axis=1)[..., None]
    return vals.transpose(0, 1, 3, 2).reshape(g * 512, n)
def pack4(w):
    words, scales = pack_weight(w, "e2m1")
    return words.reshape(words.shape[0], 128, -1), scales


def unpack4(words, scales):
    return unpack_weight(words.reshape(words.shape[0], 128, -1, 2), scales, "e2m1")


def planes(Y):
    n, m = Y.shape
    b = f64(bf(Y)).reshape(n // 32, 32, m)
    amax = np.abs(b).max(1)
    byte = np.clip(np.where(amax > 0, np.frexp(amax)[1] - 1 + 127 - 7, 1), 1, 254)
    codes = (b * np.exp2(127.0 - byte)[:, None, :]).reshape(n, m).astype(np.float32).astype(ml_dtypes.float8_e4m3fn).view(np.uint8)
    words = codes.reshape(n // 512, 128, 4, m).transpose(0, 1, 3, 2)
    return np.ascontiguousarray(words), np.ascontiguousarray(byte.astype(np.uint8).reshape(n // 512, 16, m))


NF, NC, V = 1536, 512, 1024

A_SHAPE = (NF, NF)


def setup_inputs():
    s = mx_kscale(NF)
    q = mx_kscale(NF)
    t = mx_kscale(NF)
    AT = np.random.randn(*A_SHAPE) / np.sqrt(NF)
    a_words, a_scales = pack4(AT * s[:, None] * t[None, :])
    u_words, u_scales = pack_weight(0.5 * np.random.randn(NF, V) / s[:, None], "e4m3")
    return {
        "a_words": a_words, "a_scales": a_scales,
        "u_words": u_words, "u_scales": u_scales,
        "F": bf(0.5 * np.random.randn(NF, V) * t[:, None]),
        "T": bf(0.12 * np.random.randn(NC, NF) * q[None, :]),
        "S": bf(np.random.randn(NF, NF) / np.sqrt(NF) / q[:, None]),
        "w": bf(np.exp(0.2 * np.random.randn(NF)) / t),
        "C": bf(np.random.randn(NC, V)),
        "h": bf(0.4 * np.exp(0.8 * np.random.randn(NC))),
    }


def reference(a_words, a_scales, u_words, u_scales, F, T, S, w, C, h):
    AT = unpack4(a_words, a_scales)
    U = unpack_weight(u_words, u_scales, "e4m3")
    D = f64(F) - (AT.T @ U)
    R = (mxq(f64(T), 1, "e4m3") @ mxq(f64(S), 0, "e4m3")) * f64(w)[None, :]
    y = ((mxq(R, 1, "e4m3") @ mxq(D, 0, "e4m3")) + f64(C)) * f64(h)[:, None]
    Y = y.reshape(NC, V)
    words, scales = planes(Y)
    return y, words, scales

@@ -1,0 +1,446 @@
+from contextlib import ExitStack
+
+import concourse.mybir as mybir
+from concourse.masks import make_identity
+
+NF, NC, NV = 1536, 512, 1024
+FLOPS = 2 * (NF * NF * NV + NC * NF * NF + NC * NF * NV)
+
+F32 = mybir.dt.float32
+BF16 = mybir.dt.bfloat16
+I32 = mybir.dt.int32
+U32 = mybir.dt.uint32
+U8 = mybir.dt.uint8
+FP8X4 = mybir.dt.float8_e4m3fn_x4
+FP4X4 = mybir.dt.float4_e2m1fn_x4
+ALU = mybir.AluOpType
+COPY = mybir.ActivationFunctionType.Copy
+
+P = 128
+SLOTS = 4
+KP = P * SLOTS
+G = NF // KP
+HALF = 512
+QUART = 256
+RUN = 4
+
+
+def tile_two_grid_restricted_residual_k4_kernel(
+    tc, a_words, a_scales, u_words, u_scales, F, T, S, w, C, h, out_0, out_1, out_2
+):
+    nc = tc.nc
+    with ExitStack() as ctx:
+        keep = ctx.enter_context(tc.tile_pool(name="keep", bufs=1))
+        ring = ctx.enter_context(tc.tile_pool(name="ring", bufs=4))
+        psum = ctx.enter_context(tc.psum_pool(name="psum", bufs=8))
+        ctx.enter_context(tc.manual_schedule())
+
+        def kept(name, shape, dtype):
+            return keep.tile(shape, dtype, name=name, align_bytes=64)
+
+        def mx_operand(name, width):
+            return kept(name + "_codes", [P, width], U32), kept(name + "_scales", [P, width], U8)
+
+        def new_bank(name, shape):
+            return psum.tile(shape, F32, name=name, tag="bank")
+
+        a_raw = [kept("a_raw%d" % g, [P, G, 2 * KP], U8) for g in range(G)]
+        a_raw_scales = kept("a_raw_scales", [P, G, NF], U8)
+        a_codes = [kept("a_codes%d" % g, [P, G, 2 * KP], U8) for g in range(G)]
+        a_planes = [kept("a_planes%d" % g, [P, G, KP], U8) for g in range(G)]
+        u_codes = [kept("u_codes%d" % v, [P, G, HALF], U32) for v in range(2)]
+        u_planes = kept("u_planes", [P, G, NV], U8)
+        f_rows = [[kept("f_rows%d%d" % (g, v), [P, SLOTS, HALF], BF16) for v in range(2)] for g in range(G)]
+        t_rows = [kept("t_rows%d" % j, [P, SLOTS, KP], BF16) for j in range(G)]
+        w_runs = kept("w_runs", [P, G, 16], BF16)
+        w_cols = kept("w_cols", [P, G, SLOTS], F32)
+        h_raw = kept("h_raw", [P, SLOTS], BF16)
+        h_cols = kept("h_cols", [P, SLOTS], F32)
+        c_rows = kept("c_rows", [P, SLOTS, NV], BF16)
+        y_all = kept("y_all", [P, 4, SLOTS, QUART], F32)
+        y = [y_all[:, q] for q in range(4)]
+        ident = kept("ident", [P, P], F32)
+        t_mx = [mx_operand("t%d" % j, KP) for j in range(G)]
+        s_mx = [[mx_operand("s%d%d" % (g, j), KP) for j in range(G)] for g in range(G)]
+        r_mx = [mx_operand("r%d" % g, NC) for g in range(G)]
+        d_mx = [[mx_operand("d%d%d" % (g, v), HALF) for v in range(2)] for g in range(G)]
+        y_codes = [kept("y_codes%d" % q, [P, QUART], U32) for q in range(4)]
+        y_scales = kept("y_scales", [P, NV], U8)
+
+        s_raw, flat, packed, banks = {}, {}, {}, {}
+
+        def load_scale_rows(queue, plane, scales):
+            for q in range(4):
+                queue.dma_start(
+                    out=plane[32 * q : 32 * q + 4, :, :].bitcast(I32),
+                    in_=scales[:, 4 * q : 4 * q + 4, :].rearrange("g r n -> r g n").bitcast(I32),
+                )
+
+        def load_a(g):
+            src = a_words.rearrange("k p n -> p k n")[:, :, 2 * KP * g : 2 * KP * (g + 1)]
+            nc.sync.dma_start(out=a_raw[g][:].bitcast(I32), in_=src.bitcast(I32))
+
+        def load_u(v, passes):
+            src = u_words.rearrange("k p n t -> p k (n t)")[:, passes, 4 * HALF * v : 4 * HALF * (v + 1)]
+            nc.sync.dma_start(out=u_codes[v][:, passes, :].bitcast(I32), in_=src.bitcast(I32))
+
+        def load_f(g, v):
+            src = F.rearrange("(g q t r) v -> g r q t v", g=G, t=SLOTS, r=RUN)
+            for r in range(RUN):
+                nc.sync.dma_start(out=f_rows[g][v][r:P:RUN, :, :], in_=src[g, r, :, :, HALF * v : HALF * (v + 1)])
+
+        def load_w():
+            src = w.rearrange("(g q s) -> q g s", g=G, s=16)
+            for r in range(RUN):
+                nc.sync.dma_start(out=w_runs[r:P:RUN, :, 0:13], in_=src[:, :, r : r + 13])
+
+        def load_t(j):
+            src = T.rearrange("(m t) k -> m t k", t=SLOTS)[:, :, KP * j : KP * (j + 1)]
+            nc.sync.dma_start(out=t_rows[j][:], in_=src)
+
+        def load_s(g, j):
+            s_raw[g, j] = ring.tile([P, SLOTS, KP], BF16, name="s_raw", tag="s_raw", bufs=6, align_bytes=64)
+            src = S[KP * j : KP * (j + 1), KP * g : KP * (g + 1)].rearrange("(p t) f -> p t f", t=SLOTS)
+            nc.sync.dma_start(out=s_raw[g, j][:], in_=src)
+
+        def load_c_h():
+            nc.sync.dma_start(out=h_raw[:], in_=h.rearrange("(p t) -> p t", t=SLOTS))
+            nc.sync.dma_start(out=c_rows[:], in_=C.rearrange("(p t) v -> p t v", t=SLOTS))
+
+        def copy(engine, out, in_):
+            if engine is nc.scalar:
+                nc.scalar.copy(out=out, in_=in_)
+            else:
+                engine.tensor_copy(out=out, in_=in_)
+
+        def new_packed(key, width):
+            packed[key] = ring.tile([P, width, SLOTS], BF16, name="packed", tag="packed", bufs=6, align_bytes=64)
+            return packed[key]
+
+        def deal_a(g):
+            nc.vector.tensor_copy(
+                out=a_codes[g][:].bitcast(I32).rearrange("p k (t q e) -> p k t q e", t=SLOTS, e=2),
+                in_=a_raw[g][:].bitcast(I32).rearrange("p k (q t e) -> p k t q e", t=SLOTS, e=2),
+            )
+            nc.vector.tensor_copy(
+                out=a_planes[g][:].bitcast(I32).rearrange("p k (t q) -> p k t q", t=SLOTS),
+                in_=a_raw_scales[:].bitcast(I32)[:, :, P * g : P * (g + 1)].rearrange("p k (q t) -> p k t q", t=SLOTS),
+            )
+
+        def pack_s(engine, g, j):
+            dst = new_packed(("s", g, j), KP)
+            copy(
+                engine,
+                dst[:].rearrange("p (t q r) j -> p q t j r", t=SLOTS, r=RUN),
+                s_raw[g, j][:].rearrange("p j (q t r) -> p q t j r", t=SLOTS, r=RUN),
+            )
+
+        def pack_rows(engine, key, src):
+            dst = new_packed(key, src.shape[2])
+            copy(
+                engine,
+                dst[:].rearrange("p (c i) t -> p c t i", i=4),
+                src.rearrange("p t (c i) -> p c t i", i=4),
+            )
+
+        def quantise(key, codes, scales):
+            nc.vector.quantize_mx(
+                out=codes.bitcast(FP8X4), scales=scales, in_=packed[key][:].rearrange("p c t -> p (c t)")
+            )
+
+        def quantise_s(g, j):
+            quantise(("s", g, j), s_mx[g][j][0][:], s_mx[g][j][1][:])
+
+        def turn_t(j):
+            words = t_rows[j][:].bitcast(F32)
+            for pair in range(2):
+                bank = banks["t", j, pair] = new_bank("t_bank", [P, 2, 2, P])
+                for t in range(2):
+                    for u in range(2):
+                        nc.tensor.transpose(bank[:, t, u, :], words[:, 2 * pair + t, u : KP // 2 : 2], ident[:])
+
+        def pack_t(j):
+            dst = new_packed(("t", j), KP)
+            words = dst[:].rearrange("p c t -> p (c t)").bitcast(F32).rearrange("p (t m u) -> p t m u", t=SLOTS, u=2)
+            for pair in range(2):
+                nc.scalar.copy(
+                    out=words[:, 2 * pair : 2 * pair + 2],
+                    in_=banks["t", j, pair][:].rearrange("p t u m -> p t m u"),
+                )
+
+        def quantise_t(j):
+            quantise(("t", j), t_mx[j][0][:], t_mx[j][1][:])
+
+        def new_flat(key):
+            flat[key] = ring.tile([P, SLOTS, HALF], BF16, name="flat", tag="flat", bufs=4, align_bytes=64)
+
+        def au(g, v, t):
+            bank = banks["d", g, v, t] = new_bank("au_bank", [P, HALF])
+            for k in range(G):
+                nc.tensor.matmul_mx(
+                    out=bank[:],
+                    lhsT=a_codes[g][:, k, 2 * P * t : 2 * P * (t + 1)].bitcast(FP4X4),
+                    lhsT_scale=a_planes[g][:, k, P * t : P * (t + 1)],
+                    rhs=u_codes[v][:, k, :].bitcast(FP8X4),
+                    rhs_scale=u_planes[:, k, HALF * v : HALF * (v + 1)],
+                    start=(k == 0),
+                    stop=(k == G - 1),
+                )
+
+        def residual(g, v, t):
+            if t == 0:
+                new_flat(("d", g, v))
+            nc.vector.tensor_tensor(
+                out=flat["d", g, v][:, t, :],
+                in0=f_rows[g][v][:, t, :],
+                in1=banks["d", g, v, t][:],
+                op=ALU.subtract,
+            )
+
+        def pack_d(engine, g, v):
+            pack_rows(engine, ("d", g, v), flat["d", g, v][:])
+
+        def quantise_d(g, v):
+            quantise(("d", g, v), d_mx[g][v][0][:], d_mx[g][v][1][:])
+
+        def ts(g, t):
+            bank = banks["r", g, t] = new_bank("ts_bank", [P, NC])
+            cols = slice(P * t, P * (t + 1))
+            for j in range(G):
+                nc.tensor.matmul_mx(
+                    out=bank[:],
+                    lhsT=s_mx[g][j][0][:, cols].bitcast(FP8X4),
+                    lhsT_scale=s_mx[g][j][1][:, cols],
+                    rhs=t_mx[j][0][:].bitcast(FP8X4),
+                    rhs_scale=t_mx[j][1][:],
+                    start=(j == 0),
+                    stop=(j == G - 1),
+                )
+
+        def weigh(g, t):
+            if t == 0:
+                new_flat(("r", g))
+            nc.scalar.activation(
+                out=flat["r", g][:, t, :], in_=banks["r", g, t][:], func=COPY, scale=w_cols[:, g, t : t + 1]
+            )
+
+        def pack_r(engine, g):
+            pack_rows(engine, ("r", g), flat["r", g][:])
+
+        def quantise_r(g):
+            quantise(("r", g), r_mx[g][0][:], r_mx[g][1][:])
+
+        def scale_c(t):
+            nc.vector.tensor_scalar(
+                out=y_all[:, :, t, :],
+                in0=c_rows[:, t, :].rearrange("p (q v) -> p q v", q=4),
+                scalar1=h_cols[:, t : t + 1],
+                scalar2=None,
+                op0=ALU.mult,
+            )
+
+        def rd(q, t):
+            if t % 2 == 0:
+                banks["y", q, t // 2] = new_bank("rd_bank", [P, 2, QUART])
+            rows = slice(P * t, P * (t + 1))
+            cols = slice(QUART * (q % 2), QUART * (q % 2 + 1))
+            for g in range(G):
+                nc.tensor.matmul_mx(
+                    out=banks["y", q, t // 2][:, t % 2, :],
+                    lhsT=r_mx[g][0][:, rows].bitcast(FP8X4),
+                    lhsT_scale=r_mx[g][1][:, rows],
+                    rhs=d_mx[g][q // 2][0][:, cols].bitcast(FP8X4),
+                    rhs_scale=d_mx[g][q // 2][1][:, cols],
+                    start=(g == 0),
+                    stop=(g == G - 1),
+                )
+
+        def finish_y(q, t):
+            nc.vector.scalar_tensor_tensor(
+                out=y[q][:, t, :],
+                in0=banks["y", q, t // 2][:, t % 2, :],
+                scalar=h_cols[:, t : t + 1],
+                in1=y[q][:, t, :],
+                op0=ALU.mult,
+                op1=ALU.add,
+            )
+
+        def store_y(q, slots):
+            dst = out_0.rearrange("(p t) v -> p t v", t=SLOTS)[:, slots, QUART * q : QUART * (q + 1)]
+            nc.sync.dma_start(out=dst, in_=y[q][:, slots, :])
+
+        def pack_y(engine, q):
+            pack_rows(engine, ("y", q), y[q])
+
+        def pack_y_shared(q):
+            dst = new_packed(("y", q), QUART)
+            for engine, cols in ((nc.scalar, slice(0, QUART // 2)), (nc.vector, slice(QUART // 2, QUART))):
+                copy(
+                    engine,
+                    dst[:, cols, :].rearrange("p (c i) t -> p c t i", i=4),
+                    y[q][:, :, cols].rearrange("p t (c i) -> p c t i", i=4),
+                )
+
+        def quantise_y(q):
+            quantise(("y", q), y_codes[q][:], y_scales[:, QUART * q : QUART * (q + 1)])
+            dst = out_1[0].rearrange("p m t -> p (m t)").bitcast(I32)[:, QUART * q : QUART * (q + 1)]
+            nc.sync.dma_start(out=dst, in_=y_codes[q][:].bitcast(I32))
+
+        def store_y_scales():
+            for q in range(4):
+                queue = nc.scalar if q % 2 else nc.sync
+                queue.dma_start(
+                    out=out_2[0, 4 * q : 4 * q + 4, :].bitcast(I32), in_=y_scales[32 * q : 32 * q + 4, :].bitcast(I32)
+                )
+
+        def au_group(g, v):
+            for t in range(SLOTS):
+                au(g, v, t)
+
+        def ts_group(g):
+            for t in range(SLOTS):
+                ts(g, t)
+
+        def residuals(g, v, ts_):
+            for t in ts_:
+                residual(g, v, t)
+
+        V, A = nc.vector, nc.scalar
+
+        nc.vector.memset(a_raw_scales[:].bitcast(I32), 0)
+        nc.vector.memset(u_planes[:].bitcast(I32), 0)
+        make_identity(nc, ident[:])
+        load_s(0, 0)
+        load_a(0)
+        load_scale_rows(nc.sync, a_raw_scales, a_scales)
+        load_u(0, slice(0, 2))
+        load_u(0, slice(2, 3))
+        load_scale_rows(nc.sync, u_planes, u_scales)
+        load_s(0, 1)
+        load_f(0, 0)
+        load_a(1)
+        load_t(0)
+        load_f(1, 0)
+        load_s(0, 2)
+        load_a(2)
+        load_t(1)
+        load_f(2, 0)
+        load_t(2)
+        load_w()
+        load_s(1, 0)
+        load_s(1, 1)
+        load_u(1, slice(0, 3))
+        load_f(0, 1)
+        load_s(1, 2)
+
+        pack_s(A, 0, 0)
+        deal_a(0)
+        quantise_s(0, 0)
+        load_s(2, 0)
+        pack_s(A, 0, 1)
+        load_s(2, 1)
+        au_group(0, 0)
+        residuals(0, 0, range(2))
+        deal_a(1)
+        residuals(0, 0, range(2, 4))
+        quantise_s(0, 1)
+        turn_t(0)
+        pack_t(0)
+        pack_d(A, 0, 0)
+        au_group(1, 0)
+        residuals(1, 0, range(1))
+        quantise_t(0)
+        residuals(1, 0, range(1, 2))
+        deal_a(2)
+        residuals(1, 0, range(2, 4))
+        quantise_d(0, 0)
+        pack_s(A, 0, 2)
+        load_s(2, 2)
+        load_f(1, 1)
+        load_c_h()
+        load_f(2, 1)
+        turn_t(1)
+        pack_t(1)
+        au(2, 0, 0)
+        au(2, 0, 1)
+        turn_t(2)
+        pack_t(2)
+        au(2, 0, 2)
+        au(2, 0, 3)
+        pack_d(A, 1, 0)
+        residuals(2, 0, range(1))
+        quantise_s(0, 2)
+        residuals(2, 0, range(1, 2))
+        quantise_t(1)
+        pack_s(V, 1, 0)
+        quantise_t(2)
+        nc.vector.tensor_copy(out=w_cols[:], in_=w_runs[:, :, 0:13:4])
+        residuals(2, 0, range(2, 4))
+        quantise_s(1, 0)
+        ts_group(0)
+        for t in range(4):
+            weigh(0, t)
+        pack_d(A, 2, 0)
+        pack_s(V, 1, 1)
+        quantise_d(1, 0)
+        pack_s(V, 1, 2)
+        quantise_s(1, 1)
+        au_group(0, 1)
+        residuals(0, 1, range(1))
+        quantise_s(1, 2)
+        residuals(0, 1, range(1, 3))
+        pack_s(V, 2, 0)
+        residuals(0, 1, range(3, 4))
+        pack_s(A, 2, 1)
+        quantise_s(2, 0)
+        ts_group(1)
+        pack_s(V, 2, 2)
+        quantise_s(2, 1)
+        quantise_d(2, 0)
+        quantise_s(2, 2)
+        for t in range(4):
+            weigh(1, t)
+        pack_r(V, 0)
+        ts_group(2)
+        pack_r(A, 1)
+        for t in range(4):
+            weigh(2, t)
+        nc.vector.tensor_copy(out=h_cols[:], in_=h_raw[:])
+        quantise_r(0)
+        for t in range(2):
+            scale_c(t)
+        au_group(1, 1)
+        pack_d(A, 0, 1)
+        pack_r(A, 2)
+        residuals(1, 1, range(1))
+        quantise_r(1)
+        residuals(1, 1, range(1, 2))
+        scale_c(2)
+        residuals(1, 1, range(2, 3))
+        scale_c(3)
+        residuals(1, 1, range(3, 4))
+        pack_d(A, 1, 1)
+        au_group(2, 1)
+        quantise_d(0, 1)
+        residuals(2, 1, range(2))
+        quantise_r(2)
+        residuals(2, 1, range(2, 4))
+        quantise_d(1, 1)
+        pack_d(A, 2, 1)
+        for q in range(4):
+            for t in range(4):
+                rd(q, t)
+                if t % 2:
+                    finish_y(q, t - 1)
+                    finish_y(q, t)
+                    store_y(q, slice(t - 1, t + 1))
+                if q == 1 and t == 1:
+                    quantise_d(2, 1)
+            if q > 0:
+                quantise_y(q - 1)
+            if q < 3:
+                pack_y(A, q)
+            else:
+                pack_y_shared(q)
+        quantise_y(3)
+        store_y_scales()

@@ -48,7 +48,7 @@ def tile_two_grid_restricted_residual_k4_kernel(
         a_raw_scales = kept("a_raw_scales", [P, G, NF], U8)
         a_codes = [kept("a_codes%d" % g, [P, G, 2 * KP], U8) for g in range(G)]
         a_planes = [kept("a_planes%d" % g, [P, G, KP], U8) for g in range(G)]
-        u_codes = [kept("u_codes%d" % v, [P, G, HALF], U32) for v in range(2)]
+        u_codes = [kept("u_codes%d" % q, [P, G, QUART], U32) for q in range(4)]
         u_planes = kept("u_planes", [P, G, NV], U8)
         f_rows = [[kept("f_rows%d%d" % (g, v), [P, SLOTS, HALF], BF16) for v in range(2)] for g in range(G)]
         t_rows = [kept("t_rows%d" % j, [P, SLOTS, KP], BF16) for j in range(G)]
@@ -57,32 +57,31 @@ def tile_two_grid_restricted_residual_k4_kernel(
         h_raw = kept("h_raw", [P, SLOTS], BF16)
         h_cols = kept("h_cols", [P, SLOTS], F32)
         c_rows = kept("c_rows", [P, SLOTS, NV], BF16)
-        y_all = kept("y_all", [P, 4, SLOTS, QUART], F32)
-        y = [y_all[:, q] for q in range(4)]
+        y = [kept("y%d" % q, [P, SLOTS, QUART], F32) for q in range(4)]
         ident = kept("ident", [P, P], F32)
         t_mx = [mx_operand("t%d" % j, KP) for j in range(G)]
         s_mx = [[mx_operand("s%d%d" % (g, j), KP) for j in range(G)] for g in range(G)]
         r_mx = [mx_operand("r%d" % g, NC) for g in range(G)]
-        d_mx = [[mx_operand("d%d%d" % (g, v), HALF) for v in range(2)] for g in range(G)]
+        d_mx = [[mx_operand("d%d%d" % (g, q), QUART) for q in range(4)] for g in range(G)]
         y_codes = [kept("y_codes%d" % q, [P, QUART], U32) for q in range(4)]
         y_scales = kept("y_scales", [P, NV], U8)
 
         s_raw, flat, packed, banks = {}, {}, {}, {}
 
-        def load_scale_rows(queue, plane, scales):
-            for q in range(4):
-                queue.dma_start(
-                    out=plane[32 * q : 32 * q + 4, :, :].bitcast(I32),
-                    in_=scales[:, 4 * q : 4 * q + 4, :].rearrange("g r n -> r g n").bitcast(I32),
+        def load_scale_rows(plane, scales, rows):
+            for r in rows:
+                nc.sync.dma_start(
+                    out=plane[r:P:32, :, :].bitcast(I32),
+                    in_=scales[:, r:16:4, :].rearrange("g q n -> q g n").bitcast(I32),
                 )
 
         def load_a(g):
             src = a_words.rearrange("k p n -> p k n")[:, :, 2 * KP * g : 2 * KP * (g + 1)]
             nc.sync.dma_start(out=a_raw[g][:].bitcast(I32), in_=src.bitcast(I32))
 
-        def load_u(v, passes):
-            src = u_words.rearrange("k p n t -> p k (n t)")[:, passes, 4 * HALF * v : 4 * HALF * (v + 1)]
-            nc.sync.dma_start(out=u_codes[v][:, passes, :].bitcast(I32), in_=src.bitcast(I32))
+        def load_u(q):
+            src = u_words.rearrange("k p n t -> p k (n t)")[:, :, 4 * QUART * q : 4 * QUART * (q + 1)]
+            nc.sync.dma_start(out=u_codes[q][:].bitcast(I32), in_=src.bitcast(I32))
 
         def load_f(g, v):
             src = F.rearrange("(g q t r) v -> g r q t v", g=G, t=SLOTS, r=RUN)
@@ -99,7 +98,7 @@ def tile_two_grid_restricted_residual_k4_kernel(
             nc.sync.dma_start(out=t_rows[j][:], in_=src)
 
         def load_s(g, j):
-            s_raw[g, j] = ring.tile([P, SLOTS, KP], BF16, name="s_raw", tag="s_raw", bufs=6, align_bytes=64)
+            s_raw[g, j] = ring.tile([P, SLOTS, KP], BF16, name="s_raw", tag="s_raw", bufs=7, align_bytes=64)
             src = S[KP * j : KP * (j + 1), KP * g : KP * (g + 1)].rearrange("(p t) f -> p t f", t=SLOTS)
             nc.sync.dma_start(out=s_raw[g, j][:], in_=src)
 
@@ -114,7 +113,7 @@ def tile_two_grid_restricted_residual_k4_kernel(
                 engine.tensor_copy(out=out, in_=in_)
 
         def new_packed(key, width):
-            packed[key] = ring.tile([P, width, SLOTS], BF16, name="packed", tag="packed", bufs=6, align_bytes=64)
+            packed[key] = ring.tile([P, width, SLOTS], BF16, name="packed", tag="packed", bufs=8, align_bytes=64)
             return packed[key]
 
         def deal_a(g):
@@ -172,36 +171,36 @@ def tile_two_grid_restricted_residual_k4_kernel(
             quantise(("t", j), t_mx[j][0][:], t_mx[j][1][:])
 
         def new_flat(key):
-            flat[key] = ring.tile([P, SLOTS, HALF], BF16, name="flat", tag="flat", bufs=4, align_bytes=64)
+            flat[key] = ring.tile([P, SLOTS, HALF], BF16, name="flat", tag="flat", bufs=2, align_bytes=64)
 
-        def au(g, v, t):
-            bank = banks["d", g, v, t] = new_bank("au_bank", [P, HALF])
-            for k in range(G):
-                nc.tensor.matmul_mx(
-                    out=bank[:],
-                    lhsT=a_codes[g][:, k, 2 * P * t : 2 * P * (t + 1)].bitcast(FP4X4),
-                    lhsT_scale=a_planes[g][:, k, P * t : P * (t + 1)],
-                    rhs=u_codes[v][:, k, :].bitcast(FP8X4),
-                    rhs_scale=u_planes[:, k, HALF * v : HALF * (v + 1)],
-                    start=(k == 0),
-                    stop=(k == G - 1),
-                )
+        def au(g, c):
+            bank = banks["d", g, c] = new_bank("au_bank", [P, SLOTS, P])
+            cols = slice(P * c, P * (c + 1))
+            for t in range(SLOTS):
+                for k in range(G):
+                    nc.tensor.matmul_mx(
+                        out=bank[:, t, :],
+                        lhsT=a_codes[g][:, k, 2 * P * t : 2 * P * (t + 1)].bitcast(FP4X4),
+                        lhsT_scale=a_planes[g][:, k, P * t : P * (t + 1)],
+                        rhs=u_codes[c // 2][:, k, P * (c % 2) : P * (c % 2 + 1)].bitcast(FP8X4),
+                        rhs_scale=u_planes[:, k, cols],
+                        start=(k == 0),
+                        stop=(k == G - 1),
+                    )
 
-        def residual(g, v, t):
-            if t == 0:
-                new_flat(("d", g, v))
+        def residual(g, c):
+            if c % 2 == 0:
+                new_packed(("d", g, c // 2), QUART)
+            dst = packed["d", g, c // 2][:, P * (c % 2) : P * (c % 2 + 1), :]
             nc.vector.tensor_tensor(
-                out=flat["d", g, v][:, t, :],
-                in0=f_rows[g][v][:, t, :],
-                in1=banks["d", g, v, t][:],
+                out=dst.rearrange("p (c i) t -> p c t i", i=4),
+                in0=f_rows[g][c // 4][:, :, P * (c % 4) : P * (c % 4 + 1)].rearrange("p t (c i) -> p c t i", i=4),
+                in1=banks["d", g, c][:].rearrange("p t (c i) -> p c t i", i=4),
                 op=ALU.subtract,
             )
 
-        def pack_d(engine, g, v):
-            pack_rows(engine, ("d", g, v), flat["d", g, v][:])
-
-        def quantise_d(g, v):
-            quantise(("d", g, v), d_mx[g][v][0][:], d_mx[g][v][1][:])
+        def quantise_d(g, q):
+            quantise(("d", g, q), d_mx[g][q][0][:], d_mx[g][q][1][:])
 
         def ts(g, t):
             bank = banks["r", g, t] = new_bank("ts_bank", [P, NC])
@@ -230,27 +229,26 @@ def tile_two_grid_restricted_residual_k4_kernel(
         def quantise_r(g):
             quantise(("r", g), r_mx[g][0][:], r_mx[g][1][:])
 
-        def scale_c(t):
-            nc.vector.tensor_scalar(
-                out=y_all[:, :, t, :],
-                in0=c_rows[:, t, :].rearrange("p (q v) -> p q v", q=4),
-                scalar1=h_cols[:, t : t + 1],
-                scalar2=None,
-                op0=ALU.mult,
-            )
+        def scale_c(q):
+            for t in range(SLOTS):
+                nc.scalar.activation(
+                    out=y[q][:, t, :],
+                    in_=c_rows[:, t, QUART * q : QUART * (q + 1)],
+                    func=COPY,
+                    scale=h_cols[:, t : t + 1],
+                )
 
         def rd(q, t):
             if t % 2 == 0:
                 banks["y", q, t // 2] = new_bank("rd_bank", [P, 2, QUART])
             rows = slice(P * t, P * (t + 1))
-            cols = slice(QUART * (q % 2), QUART * (q % 2 + 1))
             for g in range(G):
                 nc.tensor.matmul_mx(
                     out=banks["y", q, t // 2][:, t % 2, :],
                     lhsT=r_mx[g][0][:, rows].bitcast(FP8X4),
                     lhsT_scale=r_mx[g][1][:, rows],
-                    rhs=d_mx[g][q // 2][0][:, cols].bitcast(FP8X4),
-                    rhs_scale=d_mx[g][q // 2][1][:, cols],
+                    rhs=d_mx[g][q][0][:].bitcast(FP8X4),
+                    rhs_scale=d_mx[g][q][1][:],
                     start=(g == 0),
                     stop=(g == G - 1),
                 )
@@ -270,7 +268,7 @@ def tile_two_grid_restricted_residual_k4_kernel(
             nc.sync.dma_start(out=dst, in_=y[q][:, slots, :])
 
         def pack_y(engine, q):
-            pack_rows(engine, ("y", q), y[q])
+            pack_rows(engine, ("y", q), y[q][:])
 
         def pack_y_shared(q):
             dst = new_packed(("y", q), QUART)
@@ -293,154 +291,176 @@ def tile_two_grid_restricted_residual_k4_kernel(
                     out=out_2[0, 4 * q : 4 * q + 4, :].bitcast(I32), in_=y_scales[32 * q : 32 * q + 4, :].bitcast(I32)
                 )
 
-        def au_group(g, v):
+        def au_quarter(g, q):
+            au(g, 2 * q)
+            au(g, 2 * q + 1)
+
+        def rd_quarter(q):
             for t in range(SLOTS):
-                au(g, v, t)
+                rd(q, t)
+
+        def finish_pair(q, pair):
+            finish_y(q, 2 * pair)
+            finish_y(q, 2 * pair + 1)
+            store_y(q, slice(2 * pair, 2 * pair + 2))
+
+        def weigh_group(g):
+            for t in range(SLOTS):
+                weigh(g, t)
 
         def ts_group(g):
             for t in range(SLOTS):
                 ts(g, t)
-
-        def residuals(g, v, ts_):
-            for t in ts_:
-                residual(g, v, t)
 
         V, A = nc.vector, nc.scalar
 
         nc.vector.memset(a_raw_scales[:].bitcast(I32), 0)
         nc.vector.memset(u_planes[:].bitcast(I32), 0)
         make_identity(nc, ident[:])
-        load_s(0, 0)
         load_a(0)
-        load_scale_rows(nc.sync, a_raw_scales, a_scales)
-        load_u(0, slice(0, 2))
-        load_u(0, slice(2, 3))
-        load_scale_rows(nc.sync, u_planes, u_scales)
-        load_s(0, 1)
-        load_f(0, 0)
+        load_u(0)
+        load_scale_rows(a_raw_scales, a_scales, range(4))
+        load_scale_rows(u_planes, u_scales, range(4))
+        load_u(1)
         load_a(1)
-        load_t(0)
-        load_f(1, 0)
-        load_s(0, 2)
+        load_f(0, 0)
+        load_s(0, 0)
+        load_s(0, 1)
         load_a(2)
-        load_t(1)
-        load_f(2, 0)
-        load_t(2)
-        load_w()
+        load_f(1, 0)
         load_s(1, 0)
+        load_t(0)
+        load_f(2, 0)
+        load_s(0, 2)
+        load_t(1)
+        load_t(2)
+        load_u(2)
+        load_u(3)
         load_s(1, 1)
-        load_u(1, slice(0, 3))
         load_f(0, 1)
         load_s(1, 2)
-
-        pack_s(A, 0, 0)
-        deal_a(0)
-        quantise_s(0, 0)
+        load_w()
         load_s(2, 0)
-        pack_s(A, 0, 1)
-        load_s(2, 1)
-        au_group(0, 0)
-        residuals(0, 0, range(2))
+
+        deal_a(0)
         deal_a(1)
-        residuals(0, 0, range(2, 4))
-        quantise_s(0, 1)
-        turn_t(0)
-        pack_t(0)
-        pack_d(A, 0, 0)
-        au_group(1, 0)
-        residuals(1, 0, range(1))
-        quantise_t(0)
-        residuals(1, 0, range(1, 2))
-        deal_a(2)
-        residuals(1, 0, range(2, 4))
+        au_quarter(0, 0)
+        au_quarter(0, 1)
+        residual(0, 0)
+        residual(0, 1)
+        residual(0, 2)
         quantise_d(0, 0)
-        pack_s(A, 0, 2)
+        residual(0, 3)
+        deal_a(2)
+        quantise_d(0, 1)
+        pack_s(A, 0, 0)
+        load_s(2, 1)
+        pack_s(A, 0, 1)
         load_s(2, 2)
         load_f(1, 1)
         load_c_h()
         load_f(2, 1)
-        turn_t(1)
-        pack_t(1)
-        au(2, 0, 0)
-        au(2, 0, 1)
-        turn_t(2)
-        pack_t(2)
-        au(2, 0, 2)
-        au(2, 0, 3)
-        pack_d(A, 1, 0)
-        residuals(2, 0, range(1))
-        quantise_s(0, 2)
-        residuals(2, 0, range(1, 2))
-        quantise_t(1)
-        pack_s(V, 1, 0)
-        quantise_t(2)
-        nc.vector.tensor_copy(out=w_cols[:], in_=w_runs[:, :, 0:13:4])
-        residuals(2, 0, range(2, 4))
-        quantise_s(1, 0)
-        ts_group(0)
-        for t in range(4):
-            weigh(0, t)
-        pack_d(A, 2, 0)
-        pack_s(V, 1, 1)
+        pack_s(A, 1, 0)
+        au_quarter(1, 0)
+        au_quarter(1, 1)
+        residual(1, 0)
+        residual(1, 1)
+        quantise_s(0, 0)
+        residual(1, 2)
         quantise_d(1, 0)
-        pack_s(V, 1, 2)
+        residual(1, 3)
+        quantise_s(0, 1)
+        quantise_d(1, 1)
+        au_quarter(2, 0)
+        turn_t(0)
+        pack_t(0)
+        pack_s(A, 0, 2)
+        residual(2, 0)
+        residual(2, 1)
+        quantise_s(1, 0)
+        quantise_d(2, 0)
+        quantise_t(0)
+        au_quarter(2, 1)
+        residual(2, 2)
+        residual(2, 3)
+        turn_t(1)
+        turn_t(2)
+        pack_t(1)
+        pack_t(2)
+        pack_s(A, 1, 1)
+        pack_s(A, 1, 2)
+        quantise_s(0, 2)
+        quantise_d(2, 1)
+        quantise_t(1)
+        quantise_t(2)
+        au_quarter(0, 2)
+        au_quarter(0, 3)
+        residual(0, 4)
+        residual(0, 5)
+        residual(0, 6)
+        nc.vector.tensor_copy(out=w_cols[:], in_=w_runs[:, :, 0:13:4])
+        quantise_d(0, 2)
+        residual(0, 7)
+        ts_group(0)
+        weigh_group(0)
+        pack_r(A, 0)
         quantise_s(1, 1)
-        au_group(0, 1)
-        residuals(0, 1, range(1))
-        quantise_s(1, 2)
-        residuals(0, 1, range(1, 3))
         pack_s(V, 2, 0)
-        residuals(0, 1, range(3, 4))
-        pack_s(A, 2, 1)
+        quantise_d(0, 3)
+        quantise_s(1, 2)
+        pack_s(V, 2, 1)
         quantise_s(2, 0)
-        ts_group(1)
         pack_s(V, 2, 2)
         quantise_s(2, 1)
-        quantise_d(2, 0)
+        au_quarter(1, 2)
+        residual(1, 4)
         quantise_s(2, 2)
-        for t in range(4):
-            weigh(1, t)
-        pack_r(V, 0)
-        ts_group(2)
-        pack_r(A, 1)
-        for t in range(4):
-            weigh(2, t)
+        residual(1, 5)
         nc.vector.tensor_copy(out=h_cols[:], in_=h_raw[:])
+        ts_group(1)
+        weigh_group(1)
         quantise_r(0)
-        for t in range(2):
-            scale_c(t)
-        au_group(1, 1)
-        pack_d(A, 0, 1)
+        quantise_d(1, 2)
+        pack_r(V, 1)
+        ts_group(2)
+        weigh_group(2)
         pack_r(A, 2)
-        residuals(1, 1, range(1))
-        quantise_r(1)
-        residuals(1, 1, range(1, 2))
+        scale_c(0)
+        scale_c(1)
         scale_c(2)
-        residuals(1, 1, range(2, 3))
-        scale_c(3)
-        residuals(1, 1, range(3, 4))
-        pack_d(A, 1, 1)
-        au_group(2, 1)
-        quantise_d(0, 1)
-        residuals(2, 1, range(2))
+        quantise_r(1)
+        au_quarter(1, 3)
+        residual(1, 6)
+        residual(1, 7)
+        au_quarter(2, 2)
+        residual(2, 4)
         quantise_r(2)
-        residuals(2, 1, range(2, 4))
-        quantise_d(1, 1)
-        pack_d(A, 2, 1)
-        for q in range(4):
-            for t in range(4):
-                rd(q, t)
-                if t % 2:
-                    finish_y(q, t - 1)
-                    finish_y(q, t)
-                    store_y(q, slice(t - 1, t + 1))
-                if q == 1 and t == 1:
-                    quantise_d(2, 1)
-            if q > 0:
-                quantise_y(q - 1)
-            if q < 3:
-                pack_y(A, q)
-            else:
-                pack_y_shared(q)
+        residual(2, 5)
+        quantise_d(1, 3)
+        rd_quarter(0)
+        rd_quarter(1)
+        finish_pair(0, 0)
+        quantise_d(2, 2)
+        finish_pair(0, 1)
+        pack_y(A, 0)
+        scale_c(3)
+        au_quarter(2, 3)
+        finish_pair(1, 0)
+        finish_pair(1, 1)
+        pack_y(A, 1)
+        residual(2, 6)
+        quantise_y(0)
+        residual(2, 7)
+        rd_quarter(2)
+        quantise_d(2, 3)
+        rd_quarter(3)
+        finish_pair(2, 0)
+        quantise_y(1)
+        finish_pair(2, 1)
+        pack_y(A, 2)
+        finish_pair(3, 0)
+        finish_pair(3, 1)
+        pack_y_shared(3)
+        quantise_y(2)
         quantise_y(3)
         store_y_scales()

@@ -62,14 +62,14 @@ def tile_two_grid_restricted_residual_k4_kernel(
         t_mx = [mx_operand("t%d" % j, KP) for j in range(G)]
         s_mx = [[mx_operand("s%d%d" % (g, j), KP) for j in range(G)] for g in range(G)]
         r_mx = [mx_operand("r%d" % g, NC) for g in range(G)]
-        d_mx = [[mx_operand("d%d%d" % (g, q), QUART) for q in range(4)] for g in range(G)]
+        d_mx = [mx_operand("d%d" % g, NV) for g in range(G)]
         y_codes = [kept("y_codes%d" % q, [P, QUART], U32) for q in range(4)]
         y_scales = kept("y_scales", [P, NV], U8)
 
         s_raw, flat, packed, banks = {}, {}, {}, {}
 
-        def load_scale_rows(plane, scales, rows):
-            for r in rows:
+        def load_scale_rows(plane, scales):
+            for r in range(4):
                 nc.sync.dma_start(
                     out=plane[r:P:32, :, :].bitcast(I32),
                     in_=scales[:, r:16:4, :].rearrange("g q n -> q g n").bitcast(I32),
@@ -142,13 +142,13 @@ def tile_two_grid_restricted_residual_k4_kernel(
                 src.rearrange("p t (c i) -> p c t i", i=4),
             )
 
-        def quantise(key, codes, scales):
+        def quantise(src, codes, scales):
             nc.vector.quantize_mx(
-                out=codes.bitcast(FP8X4), scales=scales, in_=packed[key][:].rearrange("p c t -> p (c t)")
+                out=codes.bitcast(FP8X4), scales=scales, in_=src.rearrange("p c t -> p (c t)")
             )
 
         def quantise_s(g, j):
-            quantise(("s", g, j), s_mx[g][j][0][:], s_mx[g][j][1][:])
+            quantise(packed["s", g, j][:], s_mx[g][j][0][:], s_mx[g][j][1][:])
 
         def turn_t(j):
             words = t_rows[j][:].bitcast(F32)
@@ -168,7 +168,7 @@ def tile_two_grid_restricted_residual_k4_kernel(
                 )
 
         def quantise_t(j):
-            quantise(("t", j), t_mx[j][0][:], t_mx[j][1][:])
+            quantise(packed["t", j][:], t_mx[j][0][:], t_mx[j][1][:])
 
         def new_flat(key):
             flat[key] = ring.tile([P, SLOTS, HALF], BF16, name="flat", tag="flat", bufs=2, align_bytes=64)
@@ -189,18 +189,20 @@ def tile_two_grid_restricted_residual_k4_kernel(
                     )
 
         def residual(g, c):
-            if c % 2 == 0:
-                new_packed(("d", g, c // 2), QUART)
-            dst = packed["d", g, c // 2][:, P * (c % 2) : P * (c % 2 + 1), :]
+            if c % 4 == 0:
+                new_packed(("d", g, c // 4), HALF)
+            dst = packed["d", g, c // 4][:, P * (c % 4) : P * (c % 4 + 1), :]
             nc.vector.tensor_tensor(
-                out=dst.rearrange("p (c i) t -> p c t i", i=4),
-                in0=f_rows[g][c // 4][:, :, P * (c % 4) : P * (c % 4 + 1)].rearrange("p t (c i) -> p c t i", i=4),
-                in1=banks["d", g, c][:].rearrange("p t (c i) -> p c t i", i=4),
+                out=dst.rearrange("p (c i) t -> p c t i", i=2),
+                in0=f_rows[g][c // 4][:, :, P * (c % 4) : P * (c % 4 + 1)].rearrange("p t (c i) -> p c t i", i=2),
+                in1=banks["d", g, c][:].rearrange("p t (c i) -> p c t i", i=2),
                 op=ALU.subtract,
             )
 
-        def quantise_d(g, q):
-            quantise(("d", g, q), d_mx[g][q][0][:], d_mx[g][q][1][:])
+        def quantise_d(g, first, last):
+            cols = slice(QUART * first, QUART * last)
+            src = packed["d", g, first // 2][:, QUART * (first % 2) : QUART * (first % 2 + last - first), :]
+            quantise(src, d_mx[g][0][:, cols], d_mx[g][1][:, cols])
 
         def ts(g, t):
             bank = banks["r", g, t] = new_bank("ts_bank", [P, NC])
@@ -227,7 +229,7 @@ def tile_two_grid_restricted_residual_k4_kernel(
             pack_rows(engine, ("r", g), flat["r", g][:])
 
         def quantise_r(g):
-            quantise(("r", g), r_mx[g][0][:], r_mx[g][1][:])
+            quantise(packed["r", g][:], r_mx[g][0][:], r_mx[g][1][:])
 
         def scale_c(q):
             for t in range(SLOTS):
@@ -247,8 +249,8 @@ def tile_two_grid_restricted_residual_k4_kernel(
                     out=banks["y", q, t // 2][:, t % 2, :],
                     lhsT=r_mx[g][0][:, rows].bitcast(FP8X4),
                     lhsT_scale=r_mx[g][1][:, rows],
-                    rhs=d_mx[g][q][0][:].bitcast(FP8X4),
-                    rhs_scale=d_mx[g][q][1][:],
+                    rhs=d_mx[g][0][:, QUART * q : QUART * (q + 1)].bitcast(FP8X4),
+                    rhs_scale=d_mx[g][1][:, QUART * q : QUART * (q + 1)],
                     start=(g == 0),
                     stop=(g == G - 1),
                 )
@@ -280,7 +282,7 @@ def tile_two_grid_restricted_residual_k4_kernel(
                 )
 
         def quantise_y(q):
-            quantise(("y", q), y_codes[q][:], y_scales[:, QUART * q : QUART * (q + 1)])
+            quantise(packed["y", q][:], y_codes[q][:], y_scales[:, QUART * q : QUART * (q + 1)])
             dst = out_1[0].rearrange("p m t -> p (m t)").bitcast(I32)[:, QUART * q : QUART * (q + 1)]
             nc.sync.dma_start(out=dst, in_=y_codes[q][:].bitcast(I32))
 
@@ -319,8 +321,8 @@ def tile_two_grid_restricted_residual_k4_kernel(
         make_identity(nc, ident[:])
         load_a(0)
         load_u(0)
-        load_scale_rows(a_raw_scales, a_scales, range(4))
-        load_scale_rows(u_planes, u_scales, range(4))
+        load_scale_rows(a_raw_scales, a_scales)
+        load_scale_rows(u_planes, u_scales)
         load_u(1)
         load_a(1)
         load_f(0, 0)
@@ -349,10 +351,9 @@ def tile_two_grid_restricted_residual_k4_kernel(
         residual(0, 0)
         residual(0, 1)
         residual(0, 2)
-        quantise_d(0, 0)
         residual(0, 3)
         deal_a(2)
-        quantise_d(0, 1)
+        quantise_d(0, 0, 2)
         pack_s(A, 0, 0)
         load_s(2, 1)
         pack_s(A, 0, 1)
@@ -367,10 +368,9 @@ def tile_two_grid_restricted_residual_k4_kernel(
         residual(1, 1)
         quantise_s(0, 0)
         residual(1, 2)
-        quantise_d(1, 0)
         residual(1, 3)
         quantise_s(0, 1)
-        quantise_d(1, 1)
+        quantise_d(1, 0, 2)
         au_quarter(2, 0)
         turn_t(0)
         pack_t(0)
@@ -378,7 +378,6 @@ def tile_two_grid_restricted_residual_k4_kernel(
         residual(2, 0)
         residual(2, 1)
         quantise_s(1, 0)
-        quantise_d(2, 0)
         quantise_t(0)
         au_quarter(2, 1)
         residual(2, 2)
@@ -390,7 +389,7 @@ def tile_two_grid_restricted_residual_k4_kernel(
         pack_s(A, 1, 1)
         pack_s(A, 1, 2)
         quantise_s(0, 2)
-        quantise_d(2, 1)
+        quantise_d(2, 0, 2)
         quantise_t(1)
         quantise_t(2)
         au_quarter(0, 2)
@@ -398,15 +397,14 @@ def tile_two_grid_restricted_residual_k4_kernel(
         residual(0, 4)
         residual(0, 5)
         residual(0, 6)
-        nc.vector.tensor_copy(out=w_cols[:], in_=w_runs[:, :, 0:13:4])
-        quantise_d(0, 2)
         residual(0, 7)
+        nc.scalar.copy(out=w_cols[:], in_=w_runs[:, :, 0:13:4])
         ts_group(0)
         weigh_group(0)
         pack_r(A, 0)
         quantise_s(1, 1)
         pack_s(V, 2, 0)
-        quantise_d(0, 3)
+        quantise_d(0, 2, 4)
         quantise_s(1, 2)
         pack_s(V, 2, 1)
         quantise_s(2, 0)
@@ -416,11 +414,10 @@ def tile_two_grid_restricted_residual_k4_kernel(
         residual(1, 4)
         quantise_s(2, 2)
         residual(1, 5)
-        nc.vector.tensor_copy(out=h_cols[:], in_=h_raw[:])
+        nc.scalar.copy(out=h_cols[:], in_=h_raw[:])
         ts_group(1)
         weigh_group(1)
         quantise_r(0)
-        quantise_d(1, 2)
         pack_r(V, 1)
         ts_group(2)
         weigh_group(2)
@@ -436,11 +433,11 @@ def tile_two_grid_restricted_residual_k4_kernel(
         residual(2, 4)
         quantise_r(2)
         residual(2, 5)
-        quantise_d(1, 3)
+        quantise_d(1, 2, 4)
         rd_quarter(0)
         rd_quarter(1)
         finish_pair(0, 0)
-        quantise_d(2, 2)
+        quantise_d(2, 2, 3)
         finish_pair(0, 1)
         pack_y(A, 0)
         scale_c(3)
@@ -452,7 +449,7 @@ def tile_two_grid_restricted_residual_k4_kernel(
         quantise_y(0)
         residual(2, 7)
         rd_quarter(2)
-        quantise_d(2, 3)
+        quantise_d(2, 3, 4)
         rd_quarter(3)
         finish_pair(2, 0)
         quantise_y(1)

from contextlib import ExitStack

import concourse.mybir as mybir
from concourse.masks import make_identity

NF, NC, NV = 1536, 512, 1024
FLOPS = 2 * (NF * NF * NV + NC * NF * NF + NC * NF * NV)

F32 = mybir.dt.float32
BF16 = mybir.dt.bfloat16
I32 = mybir.dt.int32
U32 = mybir.dt.uint32
U8 = mybir.dt.uint8
FP8X4 = mybir.dt.float8_e4m3fn_x4
FP4X4 = mybir.dt.float4_e2m1fn_x4
ALU = mybir.AluOpType
COPY = mybir.ActivationFunctionType.Copy

P = 128
SLOTS = 4
KP = P * SLOTS
G = NF // KP
HALF = 512
QUART = 256
RUN = 4


def tile_two_grid_restricted_residual_k4_kernel(
    tc, a_words, a_scales, u_words, u_scales, F, T, S, w, C, h, out_0, out_1, out_2
):
    nc = tc.nc
    with ExitStack() as ctx:
        keep = ctx.enter_context(tc.tile_pool(name="keep", bufs=1))
        ring = ctx.enter_context(tc.tile_pool(name="ring", bufs=4))
        psum = ctx.enter_context(tc.psum_pool(name="psum", bufs=8))
        ctx.enter_context(tc.manual_schedule())

        def kept(name, shape, dtype):
            return keep.tile(shape, dtype, name=name, align_bytes=64)

        def mx_operand(name, width):
            return kept(name + "_codes", [P, width], U32), kept(name + "_scales", [P, width], U8)

        def new_bank(name, shape):
            return psum.tile(shape, F32, name=name, tag="bank")

        a_raw = [kept("a_raw%d" % g, [P, G, 2 * KP], U8) for g in range(G)]
        a_raw_scales = kept("a_raw_scales", [P, G, NF], U8)
        a_codes = [kept("a_codes%d" % g, [P, G, 2 * KP], U8) for g in range(G)]
        a_planes = [kept("a_planes%d" % g, [P, G, KP], U8) for g in range(G)]
        u_codes = [kept("u_codes%d" % q, [P, G, QUART], U32) for q in range(4)]
        u_planes = kept("u_planes", [P, G, NV], U8)
        f_rows = [[kept("f_rows%d%d" % (g, v), [P, SLOTS, HALF], BF16) for v in range(2)] for g in range(G)]
        t_rows = [kept("t_rows%d" % j, [P, SLOTS, KP], BF16) for j in range(G)]
        w_runs = kept("w_runs", [P, G, 16], BF16)
        w_cols = kept("w_cols", [P, G, SLOTS], F32)
        h_raw = kept("h_raw", [P, SLOTS], BF16)
        h_cols = kept("h_cols", [P, SLOTS], F32)
        c_rows = kept("c_rows", [P, SLOTS, NV], BF16)
        y = [kept("y%d" % q, [P, SLOTS, QUART], F32) for q in range(4)]
        ident = kept("ident", [P, P], F32)
        t_mx = [mx_operand("t%d" % j, KP) for j in range(G)]
        s_mx = [[mx_operand("s%d%d" % (g, j), KP) for j in range(G)] for g in range(G)]
        r_mx = [mx_operand("r%d" % g, NC) for g in range(G)]
        d_mx = [mx_operand("d%d" % g, NV) for g in range(G)]
        y_codes = [kept("y_codes%d" % q, [P, QUART], U32) for q in range(4)]
        y_scales = kept("y_scales", [P, NV], U8)

        s_raw, flat, packed, banks = {}, {}, {}, {}

        def load_scale_rows(plane, scales):
            for r in range(4):
                nc.sync.dma_start(
                    out=plane[r:P:32, :, :].bitcast(I32),
                    in_=scales[:, r:16:4, :].rearrange("g q n -> q g n").bitcast(I32),
                )

        def load_a(g):
            src = a_words.rearrange("k p n -> p k n")[:, :, 2 * KP * g : 2 * KP * (g + 1)]
            nc.sync.dma_start(out=a_raw[g][:].bitcast(I32), in_=src.bitcast(I32))

        def load_u(q):
            src = u_words.rearrange("k p n t -> p k (n t)")[:, :, 4 * QUART * q : 4 * QUART * (q + 1)]
            nc.sync.dma_start(out=u_codes[q][:].bitcast(I32), in_=src.bitcast(I32))

        def load_f(g, v):
            src = F.rearrange("(g q t r) v -> g r q t v", g=G, t=SLOTS, r=RUN)
            for r in range(RUN):
                nc.sync.dma_start(out=f_rows[g][v][r:P:RUN, :, :], in_=src[g, r, :, :, HALF * v : HALF * (v + 1)])

        def load_w():
            src = w.rearrange("(g q s) -> q g s", g=G, s=16)
            for r in range(RUN):
                nc.sync.dma_start(out=w_runs[r:P:RUN, :, 0:13], in_=src[:, :, r : r + 13])

        def load_t(j):
            src = T.rearrange("(m t) k -> m t k", t=SLOTS)[:, :, KP * j : KP * (j + 1)]
            nc.sync.dma_start(out=t_rows[j][:], in_=src)

        def load_s(g, j):
            s_raw[g, j] = ring.tile([P, SLOTS, KP], BF16, name="s_raw", tag="s_raw", bufs=7, align_bytes=64)
            src = S[KP * j : KP * (j + 1), KP * g : KP * (g + 1)].rearrange("(p t) f -> p t f", t=SLOTS)
            nc.sync.dma_start(out=s_raw[g, j][:], in_=src)

        def load_c_h():
            nc.sync.dma_start(out=h_raw[:], in_=h.rearrange("(p t) -> p t", t=SLOTS))
            nc.sync.dma_start(out=c_rows[:], in_=C.rearrange("(p t) v -> p t v", t=SLOTS))

        def copy(engine, out, in_):
            if engine is nc.scalar:
                nc.scalar.copy(out=out, in_=in_)
            else:
                engine.tensor_copy(out=out, in_=in_)

        def new_packed(key, width):
            packed[key] = ring.tile([P, width, SLOTS], BF16, name="packed", tag="packed", bufs=8, align_bytes=64)
            return packed[key]

        def deal_a(g):
            nc.vector.tensor_copy(
                out=a_codes[g][:].bitcast(I32).rearrange("p k (t q e) -> p k t q e", t=SLOTS, e=2),
                in_=a_raw[g][:].bitcast(I32).rearrange("p k (q t e) -> p k t q e", t=SLOTS, e=2),
            )
            nc.vector.tensor_copy(
                out=a_planes[g][:].bitcast(I32).rearrange("p k (t q) -> p k t q", t=SLOTS),
                in_=a_raw_scales[:].bitcast(I32)[:, :, P * g : P * (g + 1)].rearrange("p k (q t) -> p k t q", t=SLOTS),
            )

        def pack_s(engine, g, j):
            dst = new_packed(("s", g, j), KP)
            copy(
                engine,
                dst[:].rearrange("p (t q r) j -> p q t j r", t=SLOTS, r=RUN),
                s_raw[g, j][:].rearrange("p j (q t r) -> p q t j r", t=SLOTS, r=RUN),
            )

        def pack_rows(engine, key, src):
            dst = new_packed(key, src.shape[2])
            copy(
                engine,
                dst[:].rearrange("p (c i) t -> p c t i", i=4),
                src.rearrange("p t (c i) -> p c t i", i=4),
            )

        def quantise(src, codes, scales):
            nc.vector.quantize_mx(
                out=codes.bitcast(FP8X4), scales=scales, in_=src.rearrange("p c t -> p (c t)")
            )

        def quantise_s(g, j):
            quantise(packed["s", g, j][:], s_mx[g][j][0][:], s_mx[g][j][1][:])

        def turn_t(j):
            words = t_rows[j][:].bitcast(F32)
            for pair in range(2):
                bank = banks["t", j, pair] = new_bank("t_bank", [P, 2, 2, P])
                for t in range(2):
                    for u in range(2):
                        nc.tensor.transpose(bank[:, t, u, :], words[:, 2 * pair + t, u : KP // 2 : 2], ident[:])

        def pack_t(j):
            dst = new_packed(("t", j), KP)
            words = dst[:].rearrange("p c t -> p (c t)").bitcast(F32).rearrange("p (t m u) -> p t m u", t=SLOTS, u=2)
            for pair in range(2):
                nc.scalar.copy(
                    out=words[:, 2 * pair : 2 * pair + 2],
                    in_=banks["t", j, pair][:].rearrange("p t u m -> p t m u"),
                )

        def quantise_t(j):
            quantise(packed["t", j][:], t_mx[j][0][:], t_mx[j][1][:])

        def new_flat(key):
            flat[key] = ring.tile([P, SLOTS, HALF], BF16, name="flat", tag="flat", bufs=2, align_bytes=64)

        def au(g, c):
            bank = banks["d", g, c] = new_bank("au_bank", [P, SLOTS, P])
            cols = slice(P * c, P * (c + 1))
            for t in range(SLOTS):
                for k in range(G):
                    nc.tensor.matmul_mx(
                        out=bank[:, t, :],
                        lhsT=a_codes[g][:, k, 2 * P * t : 2 * P * (t + 1)].bitcast(FP4X4),
                        lhsT_scale=a_planes[g][:, k, P * t : P * (t + 1)],
                        rhs=u_codes[c // 2][:, k, P * (c % 2) : P * (c % 2 + 1)].bitcast(FP8X4),
                        rhs_scale=u_planes[:, k, cols],
                        start=(k == 0),
                        stop=(k == G - 1),
                    )

        def residual(g, c):
            if c % 4 == 0:
                new_packed(("d", g, c // 4), HALF)
            dst = packed["d", g, c // 4][:, P * (c % 4) : P * (c % 4 + 1), :]
            nc.vector.tensor_tensor(
                out=dst.rearrange("p (c i) t -> p c t i", i=2),
                in0=f_rows[g][c // 4][:, :, P * (c % 4) : P * (c % 4 + 1)].rearrange("p t (c i) -> p c t i", i=2),
                in1=banks["d", g, c][:].rearrange("p t (c i) -> p c t i", i=2),
                op=ALU.subtract,
            )

        def quantise_d(g, first, last):
            cols = slice(QUART * first, QUART * last)
            src = packed["d", g, first // 2][:, QUART * (first % 2) : QUART * (first % 2 + last - first), :]
            quantise(src, d_mx[g][0][:, cols], d_mx[g][1][:, cols])

        def ts(g, t):
            bank = banks["r", g, t] = new_bank("ts_bank", [P, NC])
            cols = slice(P * t, P * (t + 1))
            for j in range(G):
                nc.tensor.matmul_mx(
                    out=bank[:],
                    lhsT=s_mx[g][j][0][:, cols].bitcast(FP8X4),
                    lhsT_scale=s_mx[g][j][1][:, cols],
                    rhs=t_mx[j][0][:].bitcast(FP8X4),
                    rhs_scale=t_mx[j][1][:],
                    start=(j == 0),
                    stop=(j == G - 1),
                )

        def weigh(g, t):
            if t == 0:
                new_flat(("r", g))
            nc.scalar.activation(
                out=flat["r", g][:, t, :], in_=banks["r", g, t][:], func=COPY, scale=w_cols[:, g, t : t + 1]
            )

        def pack_r(engine, g):
            pack_rows(engine, ("r", g), flat["r", g][:])

        def quantise_r(g):
            quantise(packed["r", g][:], r_mx[g][0][:], r_mx[g][1][:])

        def scale_c(q):
            for t in range(SLOTS):
                nc.scalar.activation(
                    out=y[q][:, t, :],
                    in_=c_rows[:, t, QUART * q : QUART * (q + 1)],
                    func=COPY,
                    scale=h_cols[:, t : t + 1],
                )

        def rd(q, t):
            if t % 2 == 0:
                banks["y", q, t // 2] = new_bank("rd_bank", [P, 2, QUART])
            rows = slice(P * t, P * (t + 1))
            for g in range(G):
                nc.tensor.matmul_mx(
                    out=banks["y", q, t // 2][:, t % 2, :],
                    lhsT=r_mx[g][0][:, rows].bitcast(FP8X4),
                    lhsT_scale=r_mx[g][1][:, rows],
                    rhs=d_mx[g][0][:, QUART * q : QUART * (q + 1)].bitcast(FP8X4),
                    rhs_scale=d_mx[g][1][:, QUART * q : QUART * (q + 1)],
                    start=(g == 0),
                    stop=(g == G - 1),
                )

        def finish_y(q, t):
            nc.vector.scalar_tensor_tensor(
                out=y[q][:, t, :],
                in0=banks["y", q, t // 2][:, t % 2, :],
                scalar=h_cols[:, t : t + 1],
                in1=y[q][:, t, :],
                op0=ALU.mult,
                op1=ALU.add,
            )

        def store_y(q, slots):
            dst = out_0.rearrange("(p t) v -> p t v", t=SLOTS)[:, slots, QUART * q : QUART * (q + 1)]
            nc.sync.dma_start(out=dst, in_=y[q][:, slots, :])

        def pack_y(engine, q):
            pack_rows(engine, ("y", q), y[q][:])

        def pack_y_shared(q):
            dst = new_packed(("y", q), QUART)
            for engine, cols in ((nc.scalar, slice(0, QUART // 2)), (nc.vector, slice(QUART // 2, QUART))):
                copy(
                    engine,
                    dst[:, cols, :].rearrange("p (c i) t -> p c t i", i=4),
                    y[q][:, :, cols].rearrange("p t (c i) -> p c t i", i=4),
                )

        def quantise_y(q):
            quantise(packed["y", q][:], y_codes[q][:], y_scales[:, QUART * q : QUART * (q + 1)])
            dst = out_1[0].rearrange("p m t -> p (m t)").bitcast(I32)[:, QUART * q : QUART * (q + 1)]
            nc.sync.dma_start(out=dst, in_=y_codes[q][:].bitcast(I32))

        def store_y_scales():
            for q in range(4):
                queue = nc.scalar if q % 2 else nc.sync
                queue.dma_start(
                    out=out_2[0, 4 * q : 4 * q + 4, :].bitcast(I32), in_=y_scales[32 * q : 32 * q + 4, :].bitcast(I32)
                )

        def au_quarter(g, q):
            au(g, 2 * q)
            au(g, 2 * q + 1)

        def rd_quarter(q):
            for t in range(SLOTS):
                rd(q, t)

        def finish_pair(q, pair):
            finish_y(q, 2 * pair)
            finish_y(q, 2 * pair + 1)
            store_y(q, slice(2 * pair, 2 * pair + 2))

        def weigh_group(g):
            for t in range(SLOTS):
                weigh(g, t)

        def ts_group(g):
            for t in range(SLOTS):
                ts(g, t)

        V, A = nc.vector, nc.scalar

        nc.vector.memset(a_raw_scales[:].bitcast(I32), 0)
        nc.vector.memset(u_planes[:].bitcast(I32), 0)
        make_identity(nc, ident[:])
        load_a(0)
        load_u(0)
        load_scale_rows(a_raw_scales, a_scales)
        load_scale_rows(u_planes, u_scales)
        load_u(1)
        load_a(1)
        load_f(0, 0)
        load_s(0, 0)
        load_s(0, 1)
        load_a(2)
        load_f(1, 0)
        load_s(1, 0)
        load_t(0)
        load_f(2, 0)
        load_s(0, 2)
        load_t(1)
        load_t(2)
        load_u(2)
        load_u(3)
        load_s(1, 1)
        load_f(0, 1)
        load_s(1, 2)
        load_w()
        load_s(2, 0)

        deal_a(0)
        deal_a(1)
        au_quarter(0, 0)
        au_quarter(0, 1)
        residual(0, 0)
        residual(0, 1)
        residual(0, 2)
        residual(0, 3)
        deal_a(2)
        quantise_d(0, 0, 2)
        pack_s(A, 0, 0)
        load_s(2, 1)
        pack_s(A, 0, 1)
        load_s(2, 2)
        load_f(1, 1)
        load_c_h()
        load_f(2, 1)
        pack_s(A, 1, 0)
        au_quarter(1, 0)
        au_quarter(1, 1)
        residual(1, 0)
        residual(1, 1)
        quantise_s(0, 0)
        residual(1, 2)
        residual(1, 3)
        quantise_s(0, 1)
        quantise_d(1, 0, 2)
        au_quarter(2, 0)
        turn_t(0)
        pack_t(0)
        pack_s(A, 0, 2)
        residual(2, 0)
        residual(2, 1)
        quantise_s(1, 0)
        quantise_t(0)
        au_quarter(2, 1)
        residual(2, 2)
        residual(2, 3)
        turn_t(1)
        turn_t(2)
        pack_t(1)
        pack_t(2)
        pack_s(A, 1, 1)
        pack_s(A, 1, 2)
        quantise_s(0, 2)
        quantise_d(2, 0, 2)
        quantise_t(1)
        quantise_t(2)
        au_quarter(0, 2)
        au_quarter(0, 3)
        residual(0, 4)
        residual(0, 5)
        residual(0, 6)
        residual(0, 7)
        nc.scalar.copy(out=w_cols[:], in_=w_runs[:, :, 0:13:4])
        ts_group(0)
        weigh_group(0)
        pack_r(A, 0)
        quantise_s(1, 1)
        pack_s(V, 2, 0)
        quantise_d(0, 2, 4)
        quantise_s(1, 2)
        pack_s(V, 2, 1)
        quantise_s(2, 0)
        pack_s(V, 2, 2)
        quantise_s(2, 1)
        au_quarter(1, 2)
        residual(1, 4)
        quantise_s(2, 2)
        residual(1, 5)
        nc.scalar.copy(out=h_cols[:], in_=h_raw[:])
        ts_group(1)
        weigh_group(1)
        quantise_r(0)
        pack_r(V, 1)
        ts_group(2)
        weigh_group(2)
        pack_r(A, 2)
        scale_c(0)
        scale_c(1)
        scale_c(2)
        quantise_r(1)
        au_quarter(1, 3)
        residual(1, 6)
        residual(1, 7)
        au_quarter(2, 2)
        residual(2, 4)
        quantise_r(2)
        residual(2, 5)
        quantise_d(1, 2, 4)
        rd_quarter(0)
        rd_quarter(1)
        finish_pair(0, 0)
        quantise_d(2, 2, 3)
        finish_pair(0, 1)
        pack_y(A, 0)
        scale_c(3)
        au_quarter(2, 3)
        finish_pair(1, 0)
        finish_pair(1, 1)
        pack_y(A, 1)
        residual(2, 6)
        quantise_y(0)
        residual(2, 7)
        rd_quarter(2)
        quantise_d(2, 3, 4)
        rd_quarter(3)
        finish_pair(2, 0)
        quantise_y(1)
        finish_pair(2, 1)
        pack_y(A, 2)
        finish_pair(3, 0)
        finish_pair(3, 1)
        pack_y_shared(3)
        quantise_y(2)
        quantise_y(3)
        store_y_scales()
